import numpy as np
import ml_dtypes


def mxq(x, axis, fmt="e4m3"):
    dtype, down = {"e4m3": (ml_dtypes.float8_e4m3fn, 7), "e5m2": (ml_dtypes.float8_e5m2, 14)}[fmt]
    v = np.moveaxis(np.asarray(x, np.float32).astype(ml_dtypes.bfloat16).astype(np.float64), axis, -1)
    blocks = v.reshape(v.shape[:-1] + (-1, 32))
    amax = np.abs(blocks).max(-1, keepdims=True)
    byte = np.maximum(np.where(amax > 0, np.frexp(amax)[1] - 1 + 127, 0) - down, 1)
    scale = np.exp2(byte - 127.0)
    codes = (blocks / scale).astype(np.float32).astype(dtype).astype(np.float64)
    return np.moveaxis((codes * scale).reshape(v.shape), -1, axis)


WIDE = False


def mx_kscale(k):
    if not WIDE:
        return np.ones(k)
    levels = np.array([10, -10, 5, -5, 0])
    if k % 512:
        return np.exp2(np.random.permutation(np.resize(levels, k // 32))).repeat(32)
    a = np.empty((k // 512, 16))
    for p in range(k // 512):
        a[p, :8] = np.random.permutation(np.resize(levels, 8))
        for g in range(8):
            far = levels[np.abs(levels - a[p, g]) >= 10]
            a[p, g + 8] = far[np.random.randint(len(far))]
    return np.exp2(a.ravel()).repeat(32)


def f64(x):
    return np.asarray(x).astype(np.float64)


def striped(idx):
    return np.tile(np.asarray(idx).reshape(-1, 16).T, (8, 1)).astype(np.uint16)


def unstriped(offs):
    return offs[:16].T.reshape(-1).astype(np.int64)


E2M1 = np.array([0.0, 0.5, 1.0, 1.5, 2.0, 3.0, 4.0, 6.0, -0.0, -0.5, -1.0, -1.5, -2.0, -3.0, -4.0, -6.0])


def pack_weight(w, fmt):
    k, n = w.shape
    w = f64(np.asarray(w, np.float32).astype(ml_dtypes.bfloat16)).reshape(k // 32, 32, n)
    amax = np.abs(w).max(1)
    if fmt == "e4m3":
        byte = np.frexp(amax)[1] - 1 + 127 - 7
    else:
        mant, ex = np.frexp(amax / 6.0)
        byte = np.where(mant > 0.5, ex, ex - 1) + 127
    byte = np.clip(np.where(amax > 0, byte, 1), 1, 254)
    scaled = (w * np.exp2(127.0 - byte)[:, None, :]).reshape(k, n).astype(np.float32)
    by_word = np.ascontiguousarray(scaled.reshape(k // 512, 128, 4, n).transpose(0, 1, 3, 2))
    if fmt == "e4m3":
        words = by_word.astype(ml_dtypes.float8_e4m3fn).view(np.uint8)
    else:
        c = by_word.astype(ml_dtypes.float4_e2m1fn).view(np.uint8) & 0xF
        words = (c[..., 0::2] | (c[..., 1::2] << 4)).reshape(k // 512, 128, 2 * n)
    return np.ascontiguousarray(words), np.ascontiguousarray(byte.astype(np.uint8).reshape(k // 512, 16, n))


def unpack_weight(words, scales, fmt):
    g, _, n = scales.shape
    words = np.ascontiguousarray(words).reshape(g, 128, n, -1)
    if fmt == "e4m3":
        vals = words.view(ml_dtypes.float8_e4m3fn).astype(np.float64)
    else:
        nib = np.empty((g, 128, n, 4), np.uint8)
        nib[..., 0::2] = words & 0xF
        nib[..., 1::2] = words >> 4
        vals = E2M1[nib]
    vals = vals * np.repeat(np.exp2(scales.astype(np.float64) - 127.0), 8, axis=1)[..., None]
    return vals.transpose(0, 1, 3, 2).reshape(g * 512, n)


D, E, T, I, G, U, Q = 512, 512, 4096, 1024, 64, 512, 128


def setup_inputs():
    n = np.random.standard_normal
    idx = np.random.permutation(T)[:I]
    idx2 = np.random.permutation(U)[:G]
    fd = mx_kscale(D)
    fe = mx_kscale(E)
    keysp = pack_weight(n((D, T)) / fd[:, None], "e4m3")
    valsp = pack_weight(n((E, T)) / fe[:, None], "e4m3")
    return {
        "query": (n((D, Q)) * 0.5 / np.sqrt(D) * fd[:, None]).astype(np.float32),
        "keys_words": keysp[0],
        "keys_scales": keysp[1],
        "gout": (n((E, Q)) * 1 / np.sqrt(E) * fe[:, None]).astype(np.float32),
        "vals_words": valsp[0],
        "vals_scales": valsp[1],
        "lse": (np.random.uniform(6.8, 7.2, (Q, 1))).astype(np.float32),
        "delta": (np.random.uniform(-0.3, 0.3, (Q, 1))).astype(np.float32),
        "prior": (0.4 * n((Q, U))).astype(np.float32),
        "trust": (np.random.uniform(0.5, 1.2, (Q, 1))).astype(np.float32),
        "old": (4.0 * n((Q, U))).astype(np.float32),
        "offs": striped(idx),
        "offs2": striped(idx2),
    }


def reference(query, keys_words, keys_scales, gout, vals_words, vals_scales, lse, delta, prior, trust, old, offs, offs2):
    idx = unstriped(offs)
    idx2 = unstriped(offs2)
    keysu = unpack_weight(keys_words, keys_scales, "e4m3")
    valsu = unpack_weight(vals_words, vals_scales, "e4m3")
    queryq = mxq(f64(query), 0, "e4m3")
    keysidxg = keysu[:, idx]
    a = queryq.T @ keysidxg
    b = f64(prior)[:, idx2] * f64(trust)
    br = np.repeat(b, I // G, axis=1)
    goutq = mxq(f64(gout), 0, "e4m3")
    valsidxg = valsu[:, idx]
    dp = goutq.T @ valsidxg
    ds = np.exp(a + br - f64(lse)) * (dp - f64(delta)) * 512.0
    gb = ds.reshape(Q, G, I // G).sum(axis=2) * f64(trust)
    gf = np.zeros((Q, U))
    gf[:, idx2] = gb
    y = f64(old) + gf
    return y

@@ -1,0 +1,152 @@
+from contextlib import ExitStack
+
+import concourse.mybir as mybir
+
+D, T, I, G, U, Q = 512, 4096, 1024, 64, 512, 128
+FLOPS = 2 * 2 * Q * I * D
+
+F32 = mybir.dt.float32
+BF16 = mybir.dt.bfloat16
+I32 = mybir.dt.int32
+U32 = mybir.dt.uint32
+U16 = mybir.dt.uint16
+U8 = mybir.dt.uint8
+FP8X4 = mybir.dt.float8_e4m3fn_x4
+ALU = mybir.AluOpType
+ACT = mybir.ActivationFunctionType
+
+P = 128
+PACK = 4
+PAGE = I // G
+HALF = I // 2
+LOSS_SCALE = 512.0
+VAL_PLANE = 4
+
+
+def tile_attend_gpagebias_kernel(tc, query, keys_words, keys_scales, gout, vals_words, vals_scales,
+                                  lse, delta, prior, trust, old, offs, offs2, out):
+    nc = tc.nc
+    with ExitStack() as ctx:
+        lists = ctx.enter_context(tc.tile_pool(name="lists", bufs=1))
+        sb = ctx.enter_context(tc.tile_pool(name="sb", bufs=1))
+        psum = ctx.enter_context(tc.psum_pool(name="psum", bufs=1))
+        after_key_scales = ctx.enter_context(tc.tile_pool(name="after_key_scales", bufs=1))
+        after_val_scales = ctx.enter_context(tc.tile_pool(name="after_val_scales", bufs=1))
+        after_keys = ctx.enter_context(tc.tile_pool(name="after_keys", bufs=1))
+        after_bias = ctx.enter_context(tc.tile_pool(name="after_bias", bufs=1))
+
+        slot_list = lists.tile([P, I // 16], U16, name="slot_list")
+        page_list = lists.tile([P, G // 16], U16, name="page_list")
+        key_scale_rows = after_key_scales.tile([P, T], U8, name="key_scale_rows", offset=0)
+        val_scale_rows = after_val_scales.tile([P, T], U8, name="val_scale_rows", offset=0)
+        scattered = sb.tile([P, U], F32, name="scattered")
+        nc.vector.memset(key_scale_rows[:].bitcast(I32), 0)
+        nc.vector.memset(val_scale_rows[:].bitcast(I32), 0)
+        nc.vector.memset(scattered[:], 0.0)
+
+        query_raw = sb.tile([P, PACK, Q], F32, name="query_raw")
+        gout_raw = sb.tile([P, PACK, Q], F32, name="gout_raw")
+        key_pool = after_keys.tile([P, T], U32, name="key_pool", offset=0)
+        val_pool = sb.tile([P, T], U32, name="val_pool")
+        prior_rows = sb.tile([P, U], F32, name="prior_rows")
+        nc.sync.dma_start(slot_list[:], offs)
+        nc.sync.dma_start(page_list[:], offs2)
+        nc.sync.dma_start(query_raw[:], query.rearrange("(p j) q -> p j q", j=PACK))
+        nc.sync.dma_start(key_pool[:].bitcast(I32), keys_words[0].rearrange("p n t -> p (n t)").bitcast(I32))
+        nc.sync.dma_start(gout_raw[:], gout.rearrange("(p j) q -> p j q", j=PACK))
+        nc.sync.dma_start(prior_rows[:], prior)
+        nc.sync.dma_start(val_pool[:].bitcast(I32), vals_words[0].rearrange("p n t -> p (n t)").bitcast(I32))
+        nc.scalar.dma_start(key_scale_rows[0:P:8, :].bitcast(I32), keys_scales[0].bitcast(I32))
+        nc.scalar.dma_start(val_scale_rows[VAL_PLANE:P:8, :].bitcast(I32), vals_scales[0].bitcast(I32))
+
+        lse_col = sb.tile([P, 1], F32, name="lse_col")
+        trust_col = sb.tile([P, 1], F32, name="trust_col")
+        delta_col = sb.tile([P, 1], F32, name="delta_col")
+        nc.gpsimd.dma_start(trust_col[:], trust)
+        nc.gpsimd.dma_start(lse_col[:], lse)
+        nc.gpsimd.dma_start(delta_col[:], delta)
+
+        def quantise(raw, grouped, codes, name):
+            plane = sb.tile([P, Q], U8, name=name + "_plane", align_bytes=64)
+            nc.scalar.copy(grouped[:], raw[:].rearrange("p j q -> p q j"))
+            nc.vector.quantize_mx(out=codes[:].bitcast(FP8X4), scales=plane[:],
+                                  in_=grouped[:].rearrange("p q j -> p (q j)"))
+            return plane
+
+        def gather_scales(rows, picked, first, queues, name):
+            plane = sb.tile([P, I], U8, name=name + "_plane", align_bytes=64)
+            nc.vector.tensor_copy(picked[:], rows[:].indirect(slot_list[:]))
+            nc.vector.tensor_copy(plane[:].bitcast(I32), picked[:].bitcast(I32))
+            for r in range(1, 4):
+                queues[r - 1].dma_start(plane[first + r:P:32, :].bitcast(I32),
+                                        picked[first + 8 * r:P:32, :].bitcast(I32))
+            return plane
+
+        def products(pool, words, plane, first, codes, code_plane, name):
+            banks = []
+            for h in range(2):
+                cols = slice(h * HALF // 16, (h + 1) * HALF // 16)
+                slots = slice(h * HALF, (h + 1) * HALF)
+                nc.vector.tensor_copy(words[:, slots], pool[:].indirect(slot_list[:, cols]))
+                bank = psum.tile([P, HALF], F32, name="%s_bank%d" % (name, h))
+                nc.tensor.matmul_mx(out=bank[:], lhsT=codes[:].bitcast(FP8X4), lhsT_scale=code_plane[:],
+                                    rhs=words[:, slots].bitcast(FP8X4),
+                                    rhs_scale=plane[first:P, slots], start=True, stop=True)
+                banks.append(bank)
+            return banks
+
+        key_picked = sb.tile([P, I], U8, name="key_picked")
+        key_plane = gather_scales(key_scale_rows, key_picked, 0, [nc.scalar, nc.scalar, nc.scalar], "key")
+        query_grouped = sb.tile([P, Q, PACK], BF16, name="query_grouped", align_bytes=64)
+        query_codes = after_key_scales.tile([P, Q], U32, name="query_codes", align_bytes=64, offset=1024)
+        query_plane = quantise(query_raw, query_grouped, query_codes, "query")
+        val_picked = after_key_scales.tile([P, I], U8, name="val_picked", offset=0)
+        val_plane = gather_scales(val_scale_rows, val_picked, VAL_PLANE, [nc.scalar, nc.scalar, nc.gpsimd], "val")
+        key_words = after_val_scales.tile([P, I], U32, name="key_words", align_bytes=64, offset=1024)
+        score_banks = products(key_pool, key_words, key_plane, 0, query_codes, query_plane, "score")
+        gout_grouped = after_val_scales.tile([P, Q, PACK], BF16, name="gout_grouped", align_bytes=64, offset=0)
+        gout_codes = after_keys.tile([P, Q], U32, name="gout_codes", align_bytes=64, offset=4096)
+        gout_plane = quantise(gout_raw, gout_grouped, gout_codes, "gout")
+
+        picked_prior = after_keys.tile([P, G], F32, name="picked_prior", offset=2048)
+        page_bias = after_bias.tile([P, G], F32, name="page_bias", offset=0)
+        neg_lse = sb.tile([P, 1], F32, name="neg_lse")
+        page_factor = sb.tile([P, G], F32, name="page_factor")
+        nc.vector.tensor_copy(picked_prior[:], prior_rows[:].indirect(page_list[:]))
+        nc.scalar.activation(page_bias[:], picked_prior[:], ACT.Copy, scale=trust_col[:])
+        nc.scalar.activation(neg_lse[:], lse_col[:], ACT.Copy, scale=-1.0)
+        nc.scalar.activation(page_factor[:], trust_col[:].to_broadcast([P, G]), ACT.Copy, scale=LOSS_SCALE)
+
+        old_rows = after_keys.tile([P, U], F32, name="old_rows", offset=0)
+        nc.sync.dma_start(old_rows[:], old)
+
+        weights = []
+        for h in range(2):
+            logits = sb.tile([P, G // 2, PAGE], F32, name="logits%d" % h)
+            weight = sb.tile([P, HALF], F32, name="weight%d" % h)
+            bias = page_bias[:, h * G // 2:(h + 1) * G // 2].unsqueeze(2).to_broadcast([P, G // 2, PAGE])
+            nc.vector.tensor_tensor(logits[:], score_banks[h][:].rearrange("p (g j) -> p g j", j=PAGE), bias, ALU.add)
+            nc.scalar.activation(weight[:], logits[:].rearrange("p g j -> p (g j)"), ACT.Exp, bias=neg_lse[:])
+            weights.append(weight)
+
+        val_words = after_bias.tile([P, I], U32, name="val_words", align_bytes=64, offset=0)
+        grad_banks = products(val_pool, val_words, val_plane, VAL_PLANE, gout_codes, gout_plane, "grad")
+
+        page_sums = sb.tile([P, G], F32, name="page_sums")
+        score_grads = []
+        for h in range(2):
+            score_grad = sb.tile([P, HALF], F32, name="score_grad%d" % h)
+            nc.vector.scalar_tensor_tensor(score_grad[:], grad_banks[h][:], delta_col[:], weights[h][:],
+                                           ALU.subtract, ALU.mult)
+            score_grads.append(score_grad)
+        for h in range(2):
+            nc.vector.tensor_reduce(page_sums[:, h * G // 2:(h + 1) * G // 2],
+                                    score_grads[h][:].rearrange("p (g j) -> p g j", j=PAGE),
+                                    mybir.AxisListType.X, ALU.add)
+        nc.vector.tensor_tensor(scattered[:].indirect(page_list[:]), page_sums[:], page_factor[:], ALU.mult)
+
+        for h, queue in enumerate((nc.sync, nc.scalar)):
+            cols = slice(h * U // 2, (h + 1) * U // 2)
+            result = sb.tile([P, U // 2], F32, name="result%d" % h)
+            nc.vector.tensor_tensor(result[:], scattered[:, cols], old_rows[:, cols], ALU.add)
+            queue.dma_start(out[:, cols], result[:])

@@ -20,6 +20,9 @@ PACK = 4
 PAGE = I // G
 HALF = I // 2
 LOSS_SCALE = 512.0
+ROWS = D // 32
+KEY_ROWS = P - ROWS
+VAL_ROWS = P // 2 - ROWS
 VAL_PLANE = 4
 
 
@@ -30,86 +33,82 @@ def tile_attend_gpagebias_kernel(tc, query, keys_words, keys_scales, gout, vals_
         lists = ctx.enter_context(tc.tile_pool(name="lists", bufs=1))
         sb = ctx.enter_context(tc.tile_pool(name="sb", bufs=1))
         psum = ctx.enter_context(tc.psum_pool(name="psum", bufs=1))
-        after_key_scales = ctx.enter_context(tc.tile_pool(name="after_key_scales", bufs=1))
-        after_val_scales = ctx.enter_context(tc.tile_pool(name="after_val_scales", bufs=1))
-        after_keys = ctx.enter_context(tc.tile_pool(name="after_keys", bufs=1))
-        after_bias = ctx.enter_context(tc.tile_pool(name="after_bias", bufs=1))
+        late = ctx.enter_context(tc.tile_pool(name="late", bufs=1))
 
         slot_list = lists.tile([P, I // 16], U16, name="slot_list")
         page_list = lists.tile([P, G // 16], U16, name="page_list")
-        key_scale_rows = after_key_scales.tile([P, T], U8, name="key_scale_rows", offset=0)
-        val_scale_rows = after_val_scales.tile([P, T], U8, name="val_scale_rows", offset=0)
+        key_scale_rows = late.tile([P, T], U8, name="key_scale_rows", offset=0)
+        val_scale_rows = sb.tile([P, T], U8, name="val_scale_rows")
+        key_plane = sb.tile([P, I], U8, name="key_plane", align_bytes=64)
+        val_plane = sb.tile([P, I], U8, name="val_plane", align_bytes=64)
         scattered = sb.tile([P, U], F32, name="scattered")
-        nc.vector.memset(key_scale_rows[:].bitcast(I32), 0)
-        nc.vector.memset(val_scale_rows[:].bitcast(I32), 0)
-        nc.vector.memset(scattered[:], 0.0)
+        nc.vector.memset(key_scale_rows[0:KEY_ROWS, :].bitcast(I32), 0)
+        nc.gpsimd.memset(val_scale_rows[0:VAL_ROWS, :].bitcast(I32), 0)
+        nc.gpsimd.memset(val_scale_rows[P // 2:P, :].bitcast(I32), 0)
+        nc.vector.memset(key_plane[:].bitcast(I32), 0)
+        nc.vector.memset(val_plane[:].bitcast(I32), 0)
 
         query_raw = sb.tile([P, PACK, Q], F32, name="query_raw")
-        gout_raw = sb.tile([P, PACK, Q], F32, name="gout_raw")
-        key_pool = after_keys.tile([P, T], U32, name="key_pool", offset=0)
-        val_pool = sb.tile([P, T], U32, name="val_pool")
+        key_pool = sb.tile([P, T], U32, name="key_pool", tag="keys_then_old")
         prior_rows = sb.tile([P, U], F32, name="prior_rows")
         nc.sync.dma_start(slot_list[:], offs)
-        nc.sync.dma_start(page_list[:], offs2)
+        nc.sync.dma_start(key_scale_rows[KEY_ROWS:P, :].bitcast(I32), keys_scales[0].bitcast(I32))
+        nc.sync.dma_start(val_scale_rows[VAL_ROWS:P // 2, :].bitcast(I32), vals_scales[0].bitcast(I32))
         nc.sync.dma_start(query_raw[:], query.rearrange("(p j) q -> p j q", j=PACK))
         nc.sync.dma_start(key_pool[:].bitcast(I32), keys_words[0].rearrange("p n t -> p (n t)").bitcast(I32))
-        nc.sync.dma_start(gout_raw[:], gout.rearrange("(p j) q -> p j q", j=PACK))
         nc.sync.dma_start(prior_rows[:], prior)
-        nc.sync.dma_start(val_pool[:].bitcast(I32), vals_words[0].rearrange("p n t -> p (n t)").bitcast(I32))
-        nc.scalar.dma_start(key_scale_rows[0:P:8, :].bitcast(I32), keys_scales[0].bitcast(I32))
-        nc.scalar.dma_start(val_scale_rows[VAL_PLANE:P:8, :].bitcast(I32), vals_scales[0].bitcast(I32))
+        nc.sync.dma_start(page_list[:], offs2)
 
         lse_col = sb.tile([P, 1], F32, name="lse_col")
         trust_col = sb.tile([P, 1], F32, name="trust_col")
-        delta_col = sb.tile([P, 1], F32, name="delta_col")
         nc.gpsimd.dma_start(trust_col[:], trust)
         nc.gpsimd.dma_start(lse_col[:], lse)
-        nc.gpsimd.dma_start(delta_col[:], delta)
+        nc.gpsimd.memset(scattered[:], 0.0)
 
-        def quantise(raw, grouped, codes, name):
+        def quantise(raw, name):
+            grouped = sb.tile([P, Q, PACK], BF16, name=name + "_grouped", tag=name + "_stage", align_bytes=64)
+            codes = sb.tile([P, Q], U32, name=name + "_codes", align_bytes=64)
             plane = sb.tile([P, Q], U8, name=name + "_plane", align_bytes=64)
             nc.scalar.copy(grouped[:], raw[:].rearrange("p j q -> p q j"))
             nc.vector.quantize_mx(out=codes[:].bitcast(FP8X4), scales=plane[:],
                                   in_=grouped[:].rearrange("p q j -> p (q j)"))
-            return plane
+            return codes, plane
 
-        def gather_scales(rows, picked, first, queues, name):
-            plane = sb.tile([P, I], U8, name=name + "_plane", align_bytes=64)
+        def gather_scales(rows, first_row, plane, first, name):
+            picked = sb.tile([P, I], U8, name=name + "_picked")
             nc.vector.tensor_copy(picked[:], rows[:].indirect(slot_list[:]))
-            nc.vector.tensor_copy(plane[:].bitcast(I32), picked[:].bitcast(I32))
-            for r in range(1, 4):
-                queues[r - 1].dma_start(plane[first + r:P:32, :].bitcast(I32),
-                                        picked[first + 8 * r:P:32, :].bitcast(I32))
-            return plane
+            for quad in range(4):
+                nc.sync.dma_start(plane[32 * quad + first:32 * quad + first + 4, :].bitcast(I32),
+                                  picked[first_row + 4 * quad:first_row + 4 * quad + 4, :].bitcast(I32))
 
-        def products(pool, words, plane, first, codes, code_plane, name):
-            banks = []
-            for h in range(2):
-                cols = slice(h * HALF // 16, (h + 1) * HALF // 16)
-                slots = slice(h * HALF, (h + 1) * HALF)
-                nc.vector.tensor_copy(words[:, slots], pool[:].indirect(slot_list[:, cols]))
-                bank = psum.tile([P, HALF], F32, name="%s_bank%d" % (name, h))
-                nc.tensor.matmul_mx(out=bank[:], lhsT=codes[:].bitcast(FP8X4), lhsT_scale=code_plane[:],
-                                    rhs=words[:, slots].bitcast(FP8X4),
-                                    rhs_scale=plane[first:P, slots], start=True, stop=True)
-                banks.append(bank)
-            return banks
+        def gather_words(pool, h, name, tag):
+            words = sb.tile([P, HALF], U32, name=name, tag=tag, align_bytes=64)
+            nc.vector.tensor_copy(words[:], pool[:].indirect(slot_list[:, h * HALF // 16:(h + 1) * HALF // 16]))
+            return words
 
-        key_picked = sb.tile([P, I], U8, name="key_picked")
-        key_plane = gather_scales(key_scale_rows, key_picked, 0, [nc.scalar, nc.scalar, nc.scalar], "key")
-        query_grouped = sb.tile([P, Q, PACK], BF16, name="query_grouped", align_bytes=64)
-        query_codes = after_key_scales.tile([P, Q], U32, name="query_codes", align_bytes=64, offset=1024)
-        query_plane = quantise(query_raw, query_grouped, query_codes, "query")
-        val_picked = after_key_scales.tile([P, I], U8, name="val_picked", offset=0)
-        val_plane = gather_scales(val_scale_rows, val_picked, VAL_PLANE, [nc.scalar, nc.scalar, nc.gpsimd], "val")
-        key_words = after_val_scales.tile([P, I], U32, name="key_words", align_bytes=64, offset=1024)
-        score_banks = products(key_pool, key_words, key_plane, 0, query_codes, query_plane, "score")
-        gout_grouped = after_val_scales.tile([P, Q, PACK], BF16, name="gout_grouped", align_bytes=64, offset=0)
-        gout_codes = after_keys.tile([P, Q], U32, name="gout_codes", align_bytes=64, offset=4096)
-        gout_plane = quantise(gout_raw, gout_grouped, gout_codes, "gout")
+        def product(codes, code_plane, words, plane, name):
+            bank = psum.tile([P, words.shape[1]], F32, name=name)
+            nc.tensor.matmul_mx(out=bank[:], lhsT=codes[:].bitcast(FP8X4), lhsT_scale=code_plane[:],
+                                rhs=words.bitcast(FP8X4), rhs_scale=plane, start=True, stop=True)
+            return bank
 
-        picked_prior = after_keys.tile([P, G], F32, name="picked_prior", offset=2048)
-        page_bias = after_bias.tile([P, G], F32, name="page_bias", offset=0)
+        gather_scales(key_scale_rows, KEY_ROWS, key_plane, 0, "key")
+        val_pool = late.tile([P, T], U32, name="val_pool", offset=3072)
+        gout_raw = late.tile([P, PACK, Q], F32, name="gout_raw", offset=0)
+        delta_col = late.tile([P, 1], F32, name="delta_col", offset=2048)
+        nc.sync.dma_start(val_pool[:].bitcast(I32), vals_words[0].rearrange("p n t -> p (n t)").bitcast(I32))
+        nc.sync.dma_start(gout_raw[:], gout.rearrange("(p j) q -> p j q", j=PACK))
+        nc.sync.dma_start(delta_col[:], delta)
+        query_codes, query_plane = quantise(query_raw, "query")
+        gather_scales(val_scale_rows, VAL_ROWS, val_plane, VAL_PLANE, "val")
+        score_banks = []
+        for h in range(2):
+            words = gather_words(key_pool, h, "key_words%d" % h, "key_words%d" % h)
+            score_banks.append(product(query_codes, query_plane, words[:], key_plane[:, h * HALF:(h + 1) * HALF],
+                                       "score_bank%d" % h))
+
+        picked_prior = sb.tile([P, G], F32, name="picked_prior")
+        page_bias = sb.tile([P, G], F32, name="page_bias")
         neg_lse = sb.tile([P, 1], F32, name="neg_lse")
         page_factor = sb.tile([P, G], F32, name="page_factor")
         nc.vector.tensor_copy(picked_prior[:], prior_rows[:].indirect(page_list[:]))
@@ -117,7 +116,7 @@ def tile_attend_gpagebias_kernel(tc, query, keys_words, keys_scales, gout, vals_
         nc.scalar.activation(neg_lse[:], lse_col[:], ACT.Copy, scale=-1.0)
         nc.scalar.activation(page_factor[:], trust_col[:].to_broadcast([P, G]), ACT.Copy, scale=LOSS_SCALE)
 
-        old_rows = after_keys.tile([P, U], F32, name="old_rows", offset=0)
+        old_rows = sb.tile([P, U], F32, name="old_rows", tag="keys_then_old")
         nc.sync.dma_start(old_rows[:], old)
 
         weights = []
@@ -129,16 +128,17 @@ def tile_attend_gpagebias_kernel(tc, query, keys_words, keys_scales, gout, vals_
             nc.scalar.activation(weight[:], logits[:].rearrange("p g j -> p (g j)"), ACT.Exp, bias=neg_lse[:])
             weights.append(weight)
 
-        val_words = after_bias.tile([P, I], U32, name="val_words", align_bytes=64, offset=0)
-        grad_banks = products(val_pool, val_words, val_plane, VAL_PLANE, gout_codes, gout_plane, "grad")
+        val_words = [gather_words(val_pool, 0, "val_words0", "val_words0")]
+        gout_codes, gout_plane = quantise(gout_raw, "gout")
+        val_words.append(gather_words(val_pool, 1, "val_words1", "gout_stage"))
 
         page_sums = sb.tile([P, G], F32, name="page_sums")
-        score_grads = []
-        for h in range(2):
-            score_grad = sb.tile([P, HALF], F32, name="score_grad%d" % h)
-            nc.vector.scalar_tensor_tensor(score_grad[:], grad_banks[h][:], delta_col[:], weights[h][:],
+        score_grads = [sb.tile([P, HALF], F32, name="score_grad%d" % h) for h in range(2)]
+        for h, lo, hi in ((0, 0, HALF), (1, 0, HALF // 2), (1, HALF // 2, HALF)):
+            bank = product(gout_codes, gout_plane, val_words[h][:, lo:hi],
+                           val_plane[VAL_PLANE:P, h * HALF + lo:h * HALF + hi], "grad_bank%d_%d" % (h, lo))
+            nc.vector.scalar_tensor_tensor(score_grads[h][:, lo:hi], bank[:], delta_col[:], weights[h][:, lo:hi],
                                            ALU.subtract, ALU.mult)
-            score_grads.append(score_grad)
         for h in range(2):
             nc.vector.tensor_reduce(page_sums[:, h * G // 2:(h + 1) * G // 2],
                                     score_grads[h][:].rearrange("p (g j) -> p g j", j=PAGE),

@@ -24,6 +24,7 @@ ROWS = D // 32
 KEY_ROWS = P - ROWS
 VAL_ROWS = P // 2 - ROWS
 VAL_PLANE = 4
+SCALAR_PAGES = 20
 
 
 def tile_attend_gpagebias_kernel(tc, query, keys_words, keys_scales, gout, vals_words, vals_scales,
@@ -43,10 +44,11 @@ def tile_attend_gpagebias_kernel(tc, query, keys_words, keys_scales, gout, vals_
         val_plane = sb.tile([P, I], U8, name="val_plane", align_bytes=64)
         scattered = sb.tile([P, U], F32, name="scattered")
         nc.vector.memset(key_scale_rows[0:KEY_ROWS, :].bitcast(I32), 0)
-        nc.gpsimd.memset(val_scale_rows[0:VAL_ROWS, :].bitcast(I32), 0)
-        nc.gpsimd.memset(val_scale_rows[P // 2:P, :].bitcast(I32), 0)
+        nc.vector.memset(val_scale_rows[0:VAL_ROWS, :].bitcast(I32), 0)
+        nc.vector.memset(val_scale_rows[P // 2:P, :].bitcast(I32), 0)
         nc.vector.memset(key_plane[:].bitcast(I32), 0)
         nc.vector.memset(val_plane[:].bitcast(I32), 0)
+        nc.vector.memset(scattered[:], 0.0)
 
         query_raw = sb.tile([P, PACK, Q], F32, name="query_raw")
         key_pool = sb.tile([P, T], U32, name="key_pool", tag="keys_then_old")
@@ -61,9 +63,10 @@ def tile_attend_gpagebias_kernel(tc, query, keys_words, keys_scales, gout, vals_
 
         lse_col = sb.tile([P, 1], F32, name="lse_col")
         trust_col = sb.tile([P, 1], F32, name="trust_col")
+        delta_col = sb.tile([P, 1], F32, name="delta_col")
         nc.gpsimd.dma_start(trust_col[:], trust)
         nc.gpsimd.dma_start(lse_col[:], lse)
-        nc.gpsimd.memset(scattered[:], 0.0)
+        nc.gpsimd.dma_start(delta_col[:], delta)
 
         def quantise(raw, name):
             grouped = sb.tile([P, Q, PACK], BF16, name=name + "_grouped", tag=name + "_stage", align_bytes=64)
@@ -93,12 +96,10 @@ def tile_attend_gpagebias_kernel(tc, query, keys_words, keys_scales, gout, vals_
             return bank
 
         gather_scales(key_scale_rows, KEY_ROWS, key_plane, 0, "key")
-        val_pool = late.tile([P, T], U32, name="val_pool", offset=3072)
+        val_pool = late.tile([P, T], U32, name="val_pool", offset=2048)
         gout_raw = late.tile([P, PACK, Q], F32, name="gout_raw", offset=0)
-        delta_col = late.tile([P, 1], F32, name="delta_col", offset=2048)
         nc.sync.dma_start(val_pool[:].bitcast(I32), vals_words[0].rearrange("p n t -> p (n t)").bitcast(I32))
         nc.sync.dma_start(gout_raw[:], gout.rearrange("(p j) q -> p j q", j=PACK))
-        nc.sync.dma_start(delta_col[:], delta)
         query_codes, query_plane = quantise(query_raw, "query")
         gather_scales(val_scale_rows, VAL_ROWS, val_plane, VAL_PLANE, "val")
         score_banks = []
@@ -139,9 +140,13 @@ def tile_attend_gpagebias_kernel(tc, query, keys_words, keys_scales, gout, vals_
                            val_plane[VAL_PLANE:P, h * HALF + lo:h * HALF + hi], "grad_bank%d_%d" % (h, lo))
             nc.vector.scalar_tensor_tensor(score_grads[h][:, lo:hi], bank[:], delta_col[:], weights[h][:, lo:hi],
                                            ALU.subtract, ALU.mult)
-        for h in range(2):
-            nc.vector.tensor_reduce(page_sums[:, h * G // 2:(h + 1) * G // 2],
-                                    score_grads[h][:].rearrange("p (g j) -> p g j", j=PAGE),
+        passed = sb.tile([P, SCALAR_PAGES, PAGE], F32, name="passed")
+        for g in range(SCALAR_PAGES):
+            nc.scalar.activation(passed[:, g, :], score_grads[0][:, g * PAGE:(g + 1) * PAGE], ACT.Copy,
+                                 accum_out=page_sums[:, g:g + 1])
+        for h, first in ((0, SCALAR_PAGES), (1, 0)):
+            nc.vector.tensor_reduce(page_sums[:, h * G // 2 + first:(h + 1) * G // 2],
+                                    score_grads[h][:, first * PAGE:].rearrange("p (g j) -> p g j", j=PAGE),
                                     mybir.AxisListType.X, ALU.add)
         nc.vector.tensor_tensor(scattered[:].indirect(page_list[:]), page_sums[:], page_factor[:], ALU.mult)
 

@@ -24,7 +24,7 @@ ROWS = D // 32
 KEY_ROWS = P - ROWS
 VAL_ROWS = P // 2 - ROWS
 VAL_PLANE = 4
-SCALAR_PAGES = 20
+SCALAR_PAGES = 16
 
 
 def tile_attend_gpagebias_kernel(tc, query, keys_words, keys_scales, gout, vals_words, vals_scales,
@@ -34,12 +34,11 @@ def tile_attend_gpagebias_kernel(tc, query, keys_words, keys_scales, gout, vals_
         lists = ctx.enter_context(tc.tile_pool(name="lists", bufs=1))
         sb = ctx.enter_context(tc.tile_pool(name="sb", bufs=1))
         psum = ctx.enter_context(tc.psum_pool(name="psum", bufs=1))
-        late = ctx.enter_context(tc.tile_pool(name="late", bufs=1))
 
         slot_list = lists.tile([P, I // 16], U16, name="slot_list")
         page_list = lists.tile([P, G // 16], U16, name="page_list")
-        key_scale_rows = late.tile([P, T], U8, name="key_scale_rows", offset=0)
-        val_scale_rows = sb.tile([P, T], U8, name="val_scale_rows")
+        key_scale_rows = sb.tile([P, T], U8, name="key_scale_rows", tag="key_scales_then_vals")
+        val_scale_rows = sb.tile([P, T], U8, name="val_scale_rows", tag="val_scales_then_prior")
         key_plane = sb.tile([P, I], U8, name="key_plane", align_bytes=64)
         val_plane = sb.tile([P, I], U8, name="val_plane", align_bytes=64)
         scattered = sb.tile([P, U], F32, name="scattered")
@@ -52,13 +51,13 @@ def tile_attend_gpagebias_kernel(tc, query, keys_words, keys_scales, gout, vals_
 
         query_raw = sb.tile([P, PACK, Q], F32, name="query_raw")
         key_pool = sb.tile([P, T], U32, name="key_pool", tag="keys_then_old")
-        prior_rows = sb.tile([P, U], F32, name="prior_rows")
+        gout_raw = sb.tile([P, PACK, Q], F32, name="gout_raw")
         nc.sync.dma_start(slot_list[:], offs)
         nc.sync.dma_start(key_scale_rows[KEY_ROWS:P, :].bitcast(I32), keys_scales[0].bitcast(I32))
         nc.sync.dma_start(val_scale_rows[VAL_ROWS:P // 2, :].bitcast(I32), vals_scales[0].bitcast(I32))
         nc.sync.dma_start(query_raw[:], query.rearrange("(p j) q -> p j q", j=PACK))
         nc.sync.dma_start(key_pool[:].bitcast(I32), keys_words[0].rearrange("p n t -> p (n t)").bitcast(I32))
-        nc.sync.dma_start(prior_rows[:], prior)
+        nc.sync.dma_start(gout_raw[:], gout.rearrange("(p j) q -> p j q", j=PACK))
         nc.sync.dma_start(page_list[:], offs2)
 
         lse_col = sb.tile([P, 1], F32, name="lse_col")
@@ -69,7 +68,7 @@ def tile_attend_gpagebias_kernel(tc, query, keys_words, keys_scales, gout, vals_
         nc.gpsimd.dma_start(delta_col[:], delta)
 
         def quantise(raw, name):
-            grouped = sb.tile([P, Q, PACK], BF16, name=name + "_grouped", tag=name + "_stage", align_bytes=64)
+            grouped = sb.tile([P, Q, PACK], BF16, name=name + "_grouped", align_bytes=64)
             codes = sb.tile([P, Q], U32, name=name + "_codes", align_bytes=64)
             plane = sb.tile([P, Q], U8, name=name + "_plane", align_bytes=64)
             nc.scalar.copy(grouped[:], raw[:].rearrange("p j q -> p q j"))
@@ -80,12 +79,12 @@ def tile_attend_gpagebias_kernel(tc, query, keys_words, keys_scales, gout, vals_
         def gather_scales(rows, first_row, plane, first, name):
             picked = sb.tile([P, I], U8, name=name + "_picked")
             nc.vector.tensor_copy(picked[:], rows[:].indirect(slot_list[:]))
-            for quad in range(4):
-                nc.sync.dma_start(plane[32 * quad + first:32 * quad + first + 4, :].bitcast(I32),
-                                  picked[first_row + 4 * quad:first_row + 4 * quad + 4, :].bitcast(I32))
+            for r in range(4):
+                nc.sync.dma_start(plane[first + r:P:32, :].bitcast(I32),
+                                  picked[first_row + r:first_row + ROWS:4, :].bitcast(I32))
 
-        def gather_words(pool, h, name, tag):
-            words = sb.tile([P, HALF], U32, name=name, tag=tag, align_bytes=64)
+        def gather_words(pool, h, name):
+            words = sb.tile([P, HALF], U32, name=name, align_bytes=64)
             nc.vector.tensor_copy(words[:], pool[:].indirect(slot_list[:, h * HALF // 16:(h + 1) * HALF // 16]))
             return words
 
@@ -96,42 +95,51 @@ def tile_attend_gpagebias_kernel(tc, query, keys_words, keys_scales, gout, vals_
             return bank
 
         gather_scales(key_scale_rows, KEY_ROWS, key_plane, 0, "key")
-        val_pool = late.tile([P, T], U32, name="val_pool", offset=2048)
-        gout_raw = late.tile([P, PACK, Q], F32, name="gout_raw", offset=0)
+        val_pool = sb.tile([P, T], U32, name="val_pool", tag="key_scales_then_vals")
         nc.sync.dma_start(val_pool[:].bitcast(I32), vals_words[0].rearrange("p n t -> p (n t)").bitcast(I32))
-        nc.sync.dma_start(gout_raw[:], gout.rearrange("(p j) q -> p j q", j=PACK))
         query_codes, query_plane = quantise(query_raw, "query")
         gather_scales(val_scale_rows, VAL_ROWS, val_plane, VAL_PLANE, "val")
+        prior_rows = sb.tile([P, U], F32, name="prior_rows", tag="val_scales_then_prior")
+        nc.sync.dma_start(prior_rows[:], prior)
         score_banks = []
         for h in range(2):
-            words = gather_words(key_pool, h, "key_words%d" % h, "key_words%d" % h)
+            words = gather_words(key_pool, h, "key_words%d" % h)
             score_banks.append(product(query_codes, query_plane, words[:], key_plane[:, h * HALF:(h + 1) * HALF],
                                        "score_bank%d" % h))
 
-        picked_prior = sb.tile([P, G], F32, name="picked_prior")
-        page_bias = sb.tile([P, G], F32, name="page_bias")
-        neg_lse = sb.tile([P, 1], F32, name="neg_lse")
-        page_factor = sb.tile([P, G], F32, name="page_factor")
-        nc.vector.tensor_copy(picked_prior[:], prior_rows[:].indirect(page_list[:]))
-        nc.scalar.activation(page_bias[:], picked_prior[:], ACT.Copy, scale=trust_col[:])
-        nc.scalar.activation(neg_lse[:], lse_col[:], ACT.Copy, scale=-1.0)
-        nc.scalar.activation(page_factor[:], trust_col[:].to_broadcast([P, G]), ACT.Copy, scale=LOSS_SCALE)
-
+        gout_codes, gout_plane = quantise(gout_raw, "gout")
         old_rows = sb.tile([P, U], F32, name="old_rows", tag="keys_then_old")
         nc.sync.dma_start(old_rows[:], old)
 
-        weights = []
+        neg_page_max = sb.tile([P, G], F32, name="neg_page_max")
         for h in range(2):
-            logits = sb.tile([P, G // 2, PAGE], F32, name="logits%d" % h)
-            weight = sb.tile([P, HALF], F32, name="weight%d" % h)
-            bias = page_bias[:, h * G // 2:(h + 1) * G // 2].unsqueeze(2).to_broadcast([P, G // 2, PAGE])
-            nc.vector.tensor_tensor(logits[:], score_banks[h][:].rearrange("p (g j) -> p g j", j=PAGE), bias, ALU.add)
-            nc.scalar.activation(weight[:], logits[:].rearrange("p g j -> p (g j)"), ACT.Exp, bias=neg_lse[:])
-            weights.append(weight)
+            nc.vector.tensor_reduce(neg_page_max[:, h * G // 2:(h + 1) * G // 2],
+                                    score_banks[h][:].rearrange("p (g j) -> p g j", j=PAGE),
+                                    mybir.AxisListType.X, ALU.max, negate=True)
+        weights = [sb.tile([P, HALF], F32, name="weight%d" % h) for h in range(2)]
+        for g in range(G // 2):
+            slots = slice(g * PAGE, (g + 1) * PAGE)
+            nc.scalar.activation(weights[0][:, slots], score_banks[0][:, slots], ACT.Exp, bias=neg_page_max[:, g:g + 1])
+        shifted = sb.tile([P, G // 2, PAGE], F32, name="shifted")
+        shift = neg_page_max[:, G // 2:].unsqueeze(2).to_broadcast([P, G // 2, PAGE])
+        nc.vector.tensor_tensor(shifted[:], score_banks[1][:].rearrange("p (g j) -> p g j", j=PAGE), shift, ALU.add)
+        nc.scalar.activation(weights[1][:], shifted[:].rearrange("p g j -> p (g j)"), ACT.Exp)
 
-        val_words = [gather_words(val_pool, 0, "val_words0", "val_words0")]
-        gout_codes, gout_plane = quantise(gout_raw, "gout")
-        val_words.append(gather_words(val_pool, 1, "val_words1", "gout_stage"))
+        val_words = [gather_words(val_pool, h, "val_words%d" % h) for h in range(2)]
+
+        picked_prior = sb.tile([P, G], F32, name="picked_prior")
+        top_logit = sb.tile([P, G], F32, name="top_logit")
+        top_weight = sb.tile([P, G], F32, name="top_weight")
+        page_factor = sb.tile([P, G], F32, name="page_factor")
+        neg_lse = sb.tile([P, 1], F32, name="neg_lse")
+        scaled_trust = sb.tile([P, 1], F32, name="scaled_trust")
+        nc.scalar.activation(neg_lse[:], lse_col[:], ACT.Copy, scale=-1.0)
+        nc.scalar.activation(scaled_trust[:], trust_col[:], ACT.Copy, scale=LOSS_SCALE)
+        nc.vector.tensor_copy(picked_prior[:], prior_rows[:].indirect(page_list[:]))
+        nc.vector.scalar_tensor_tensor(top_logit[:], picked_prior[:], trust_col[:], neg_page_max[:],
+                                       ALU.mult, ALU.subtract)
+        nc.scalar.activation(top_weight[:], top_logit[:], ACT.Exp, bias=neg_lse[:])
+        nc.scalar.activation(page_factor[:], top_weight[:], ACT.Copy, scale=scaled_trust[:])
 
         page_sums = sb.tile([P, G], F32, name="page_sums")
         score_grads = [sb.tile([P, HALF], F32, name="score_grad%d" % h) for h in range(2)]

@@ -34,11 +34,12 @@ def tile_attend_gpagebias_kernel(tc, query, keys_words, keys_scales, gout, vals_
         lists = ctx.enter_context(tc.tile_pool(name="lists", bufs=1))
         sb = ctx.enter_context(tc.tile_pool(name="sb", bufs=1))
         psum = ctx.enter_context(tc.psum_pool(name="psum", bufs=1))
+        late = ctx.enter_context(tc.tile_pool(name="late", bufs=1))
 
         slot_list = lists.tile([P, I // 16], U16, name="slot_list")
         page_list = lists.tile([P, G // 16], U16, name="page_list")
         key_scale_rows = sb.tile([P, T], U8, name="key_scale_rows", tag="key_scales_then_vals")
-        val_scale_rows = sb.tile([P, T], U8, name="val_scale_rows", tag="val_scales_then_prior")
+        val_scale_rows = late.tile([P, T], U8, name="val_scale_rows", offset=0)
         key_plane = sb.tile([P, I], U8, name="key_plane", align_bytes=64)
         val_plane = sb.tile([P, I], U8, name="val_plane", align_bytes=64)
         scattered = sb.tile([P, U], F32, name="scattered")
@@ -61,11 +62,7 @@ def tile_attend_gpagebias_kernel(tc, query, keys_words, keys_scales, gout, vals_
         nc.sync.dma_start(page_list[:], offs2)
 
         lse_col = sb.tile([P, 1], F32, name="lse_col")
-        trust_col = sb.tile([P, 1], F32, name="trust_col")
-        delta_col = sb.tile([P, 1], F32, name="delta_col")
-        nc.gpsimd.dma_start(trust_col[:], trust)
         nc.gpsimd.dma_start(lse_col[:], lse)
-        nc.gpsimd.dma_start(delta_col[:], delta)
 
         def quantise(raw, name):
             grouped = sb.tile([P, Q, PACK], BF16, name=name + "_grouped", align_bytes=64)
@@ -99,8 +96,12 @@ def tile_attend_gpagebias_kernel(tc, query, keys_words, keys_scales, gout, vals_
         nc.sync.dma_start(val_pool[:].bitcast(I32), vals_words[0].rearrange("p n t -> p (n t)").bitcast(I32))
         query_codes, query_plane = quantise(query_raw, "query")
         gather_scales(val_scale_rows, VAL_ROWS, val_plane, VAL_PLANE, "val")
-        prior_rows = sb.tile([P, U], F32, name="prior_rows", tag="val_scales_then_prior")
+        prior_rows = late.tile([P, U], F32, name="prior_rows", offset=0)
+        trust_col = late.tile([P, 1], F32, name="trust_col", offset=2048)
+        delta_col = late.tile([P, 1], F32, name="delta_col", offset=2080)
         nc.sync.dma_start(prior_rows[:], prior)
+        nc.sync.dma_start(trust_col[:], trust)
+        nc.sync.dma_start(delta_col[:], delta)
         score_banks = []
         for h in range(2):
             words = gather_words(key_pool, h, "key_words%d" % h)
@@ -143,11 +144,16 @@ def tile_attend_gpagebias_kernel(tc, query, keys_words, keys_scales, gout, vals_
 
         page_sums = sb.tile([P, G], F32, name="page_sums")
         score_grads = [sb.tile([P, HALF], F32, name="score_grad%d" % h) for h in range(2)]
-        for h, lo, hi in ((0, 0, HALF), (1, 0, HALF // 2), (1, HALF // 2, HALF)):
+
+        def score_gradient(h, lo, hi):
             bank = product(gout_codes, gout_plane, val_words[h][:, lo:hi],
                            val_plane[VAL_PLANE:P, h * HALF + lo:h * HALF + hi], "grad_bank%d_%d" % (h, lo))
             nc.vector.scalar_tensor_tensor(score_grads[h][:, lo:hi], bank[:], delta_col[:], weights[h][:, lo:hi],
                                            ALU.subtract, ALU.mult)
+
+        score_gradient(0, 0, HALF)
+        score_gradient(1, 0, HALF // 2)
+        score_gradient(1, HALF // 2, HALF)
         passed = sb.tile([P, SCALAR_PAGES, PAGE], F32, name="passed")
         for g in range(SCALAR_PAGES):
             nc.scalar.activation(passed[:, g, :], score_grads[0][:, g * PAGE:(g + 1) * PAGE], ACT.Copy,

from contextlib import ExitStack

import concourse.mybir as mybir

D, T, I, G, U, Q = 512, 4096, 1024, 64, 512, 128
FLOPS = 2 * 2 * Q * I * D

F32 = mybir.dt.float32
BF16 = mybir.dt.bfloat16
I32 = mybir.dt.int32
U32 = mybir.dt.uint32
U16 = mybir.dt.uint16
U8 = mybir.dt.uint8
FP8X4 = mybir.dt.float8_e4m3fn_x4
ALU = mybir.AluOpType
ACT = mybir.ActivationFunctionType

P = 128
PACK = 4
PAGE = I // G
HALF = I // 2
LOSS_SCALE = 512.0
ROWS = D // 32
KEY_ROWS = P - ROWS
VAL_ROWS = P // 2 - ROWS
VAL_PLANE = 4
SCALAR_PAGES = 16


def tile_attend_gpagebias_kernel(tc, query, keys_words, keys_scales, gout, vals_words, vals_scales,
                                  lse, delta, prior, trust, old, offs, offs2, out):
    nc = tc.nc
    with ExitStack() as ctx:
        lists = ctx.enter_context(tc.tile_pool(name="lists", bufs=1))
        sb = ctx.enter_context(tc.tile_pool(name="sb", bufs=1))
        psum = ctx.enter_context(tc.psum_pool(name="psum", bufs=1))
        late = ctx.enter_context(tc.tile_pool(name="late", bufs=1))

        slot_list = lists.tile([P, I // 16], U16, name="slot_list")
        page_list = lists.tile([P, G // 16], U16, name="page_list")
        key_scale_rows = sb.tile([P, T], U8, name="key_scale_rows", tag="key_scales_then_vals")
        val_scale_rows = late.tile([P, T], U8, name="val_scale_rows", offset=0)
        key_plane = sb.tile([P, I], U8, name="key_plane", align_bytes=64)
        val_plane = sb.tile([P, I], U8, name="val_plane", align_bytes=64)
        scattered = sb.tile([P, U], F32, name="scattered")
        nc.vector.memset(key_scale_rows[0:KEY_ROWS, :].bitcast(I32), 0)
        nc.vector.memset(val_scale_rows[0:VAL_ROWS, :].bitcast(I32), 0)
        nc.vector.memset(val_scale_rows[P // 2:P, :].bitcast(I32), 0)
        nc.vector.memset(key_plane[:].bitcast(I32), 0)
        nc.vector.memset(val_plane[:].bitcast(I32), 0)
        nc.vector.memset(scattered[:], 0.0)

        query_raw = sb.tile([P, PACK, Q], F32, name="query_raw")
        key_pool = sb.tile([P, T], U32, name="key_pool", tag="keys_then_old")
        gout_raw = sb.tile([P, PACK, Q], F32, name="gout_raw")
        nc.sync.dma_start(slot_list[:], offs)
        nc.sync.dma_start(key_scale_rows[KEY_ROWS:P, :].bitcast(I32), keys_scales[0].bitcast(I32))
        nc.sync.dma_start(val_scale_rows[VAL_ROWS:P // 2, :].bitcast(I32), vals_scales[0].bitcast(I32))
        nc.sync.dma_start(query_raw[:], query.rearrange("(p j) q -> p j q", j=PACK))
        nc.sync.dma_start(key_pool[:].bitcast(I32), keys_words[0].rearrange("p n t -> p (n t)").bitcast(I32))
        nc.sync.dma_start(gout_raw[:], gout.rearrange("(p j) q -> p j q", j=PACK))
        nc.sync.dma_start(page_list[:], offs2)

        lse_col = sb.tile([P, 1], F32, name="lse_col")
        nc.gpsimd.dma_start(lse_col[:], lse)

        def quantise(raw, name):
            grouped = sb.tile([P, Q, PACK], BF16, name=name + "_grouped", align_bytes=64)
            codes = sb.tile([P, Q], U32, name=name + "_codes", align_bytes=64)
            plane = sb.tile([P, Q], U8, name=name + "_plane", align_bytes=64)
            nc.scalar.copy(grouped[:], raw[:].rearrange("p j q -> p q j"))
            nc.vector.quantize_mx(out=codes[:].bitcast(FP8X4), scales=plane[:],
                                  in_=grouped[:].rearrange("p q j -> p (q j)"))
            return codes, plane

        def gather_scales(rows, first_row, plane, first, name):
            picked = sb.tile([P, I], U8, name=name + "_picked")
            nc.vector.tensor_copy(picked[:], rows[:].indirect(slot_list[:]))
            for r in range(4):
                nc.sync.dma_start(plane[first + r:P:32, :].bitcast(I32),
                                  picked[first_row + r:first_row + ROWS:4, :].bitcast(I32))

        def gather_words(pool, h, name):
            words = sb.tile([P, HALF], U32, name=name, align_bytes=64)
            nc.vector.tensor_copy(words[:], pool[:].indirect(slot_list[:, h * HALF // 16:(h + 1) * HALF // 16]))
            return words

        def product(codes, code_plane, words, plane, name):
            bank = psum.tile([P, words.shape[1]], F32, name=name)
            nc.tensor.matmul_mx(out=bank[:], lhsT=codes[:].bitcast(FP8X4), lhsT_scale=code_plane[:],
                                rhs=words.bitcast(FP8X4), rhs_scale=plane, start=True, stop=True)
            return bank

        gather_scales(key_scale_rows, KEY_ROWS, key_plane, 0, "key")
        val_pool = sb.tile([P, T], U32, name="val_pool", tag="key_scales_then_vals")
        nc.sync.dma_start(val_pool[:].bitcast(I32), vals_words[0].rearrange("p n t -> p (n t)").bitcast(I32))
        query_codes, query_plane = quantise(query_raw, "query")
        gather_scales(val_scale_rows, VAL_ROWS, val_plane, VAL_PLANE, "val")
        prior_rows = late.tile([P, U], F32, name="prior_rows", offset=0)
        trust_col = late.tile([P, 1], F32, name="trust_col", offset=2048)
        delta_col = late.tile([P, 1], F32, name="delta_col", offset=2080)
        nc.sync.dma_start(prior_rows[:], prior)
        nc.sync.dma_start(trust_col[:], trust)
        nc.sync.dma_start(delta_col[:], delta)
        score_banks = []
        for h in range(2):
            words = gather_words(key_pool, h, "key_words%d" % h)
            score_banks.append(product(query_codes, query_plane, words[:], key_plane[:, h * HALF:(h + 1) * HALF],
                                       "score_bank%d" % h))

        gout_codes, gout_plane = quantise(gout_raw, "gout")
        old_rows = sb.tile([P, U], F32, name="old_rows", tag="keys_then_old")
        nc.sync.dma_start(old_rows[:], old)

        neg_page_max = sb.tile([P, G], F32, name="neg_page_max")
        for h in range(2):
            nc.vector.tensor_reduce(neg_page_max[:, h * G // 2:(h + 1) * G // 2],
                                    score_banks[h][:].rearrange("p (g j) -> p g j", j=PAGE),
                                    mybir.AxisListType.X, ALU.max, negate=True)
        weights = [sb.tile([P, HALF], F32, name="weight%d" % h) for h in range(2)]
        for g in range(G // 2):
            slots = slice(g * PAGE, (g + 1) * PAGE)
            nc.scalar.activation(weights[0][:, slots], score_banks[0][:, slots], ACT.Exp, bias=neg_page_max[:, g:g + 1])
        shifted = sb.tile([P, G // 2, PAGE], F32, name="shifted")
        shift = neg_page_max[:, G // 2:].unsqueeze(2).to_broadcast([P, G // 2, PAGE])
        nc.vector.tensor_tensor(shifted[:], score_banks[1][:].rearrange("p (g j) -> p g j", j=PAGE), shift, ALU.add)
        nc.scalar.activation(weights[1][:], shifted[:].rearrange("p g j -> p (g j)"), ACT.Exp)

        val_words = [gather_words(val_pool, h, "val_words%d" % h) for h in range(2)]

        picked_prior = sb.tile([P, G], F32, name="picked_prior")
        top_logit = sb.tile([P, G], F32, name="top_logit")
        top_weight = sb.tile([P, G], F32, name="top_weight")
        page_factor = sb.tile([P, G], F32, name="page_factor")
        neg_lse = sb.tile([P, 1], F32, name="neg_lse")
        scaled_trust = sb.tile([P, 1], F32, name="scaled_trust")
        nc.scalar.activation(neg_lse[:], lse_col[:], ACT.Copy, scale=-1.0)
        nc.scalar.activation(scaled_trust[:], trust_col[:], ACT.Copy, scale=LOSS_SCALE)
        nc.vector.tensor_copy(picked_prior[:], prior_rows[:].indirect(page_list[:]))
        nc.vector.scalar_tensor_tensor(top_logit[:], picked_prior[:], trust_col[:], neg_page_max[:],
                                       ALU.mult, ALU.subtract)
        nc.scalar.activation(top_weight[:], top_logit[:], ACT.Exp, bias=neg_lse[:])
        nc.scalar.activation(page_factor[:], top_weight[:], ACT.Copy, scale=scaled_trust[:])

        page_sums = sb.tile([P, G], F32, name="page_sums")
        score_grads = [sb.tile([P, HALF], F32, name="score_grad%d" % h) for h in range(2)]

        def score_gradient(h, lo, hi):
            bank = product(gout_codes, gout_plane, val_words[h][:, lo:hi],
                           val_plane[VAL_PLANE:P, h * HALF + lo:h * HALF + hi], "grad_bank%d_%d" % (h, lo))
            nc.vector.scalar_tensor_tensor(score_grads[h][:, lo:hi], bank[:], delta_col[:], weights[h][:, lo:hi],
                                           ALU.subtract, ALU.mult)

        score_gradient(0, 0, HALF)
        score_gradient(1, 0, HALF // 2)
        score_gradient(1, HALF // 2, HALF)
        passed = sb.tile([P, SCALAR_PAGES, PAGE], F32, name="passed")
        for g in range(SCALAR_PAGES):
            nc.scalar.activation(passed[:, g, :], score_grads[0][:, g * PAGE:(g + 1) * PAGE], ACT.Copy,
                                 accum_out=page_sums[:, g:g + 1])
        for h, first in ((0, SCALAR_PAGES), (1, 0)):
            nc.vector.tensor_reduce(page_sums[:, h * G // 2 + first:(h + 1) * G // 2],
                                    score_grads[h][:, first * PAGE:].rearrange("p (g j) -> p g j", j=PAGE),
                                    mybir.AxisListType.X, ALU.add)
        nc.vector.tensor_tensor(scattered[:].indirect(page_list[:]), page_sums[:], page_factor[:], ALU.mult)

        for h, queue in enumerate((nc.sync, nc.scalar)):
            cols = slice(h * U // 2, (h + 1) * U // 2)
            result = sb.tile([P, U // 2], F32, name="result%d" % h)
            nc.vector.tensor_tensor(result[:], scattered[:, cols], old_rows[:, cols], ALU.add)
            queue.dma_start(out[:, cols], result[:])
